import numpy as np
import ml_dtypes


def mxq(x, axis, fmt="e4m3"):
    dtype, down = {"e4m3": (ml_dtypes.float8_e4m3fn, 7), "e5m2": (ml_dtypes.float8_e5m2, 14)}[fmt]
    v = np.moveaxis(np.asarray(x, np.float32).astype(ml_dtypes.bfloat16).astype(np.float64), axis, -1)
    blocks = v.reshape(v.shape[:-1] + (-1, 32))
    amax = np.abs(blocks).max(-1, keepdims=True)
    byte = np.maximum(np.where(amax > 0, np.frexp(amax)[1] - 1 + 127, 0) - down, 1)
    scale = np.exp2(byte - 127.0)
    codes = (blocks / scale).astype(np.float32).astype(dtype).astype(np.float64)
    return np.moveaxis((codes * scale).reshape(v.shape), -1, axis)


WIDE = False


def mx_kscale(k):
    if not WIDE:
        return np.ones(k)
    levels = np.array([10, -10, 5, -5, 0])
    if k % 512:
        return np.exp2(np.random.permutation(np.resize(levels, k // 32))).repeat(32)
    a = np.empty((k // 512, 16))
    for p in range(k // 512):
        a[p, :8] = np.random.permutation(np.resize(levels, 8))
        for g in range(8):
            far = levels[np.abs(levels - a[p, g]) >= 10]
            a[p, g + 8] = far[np.random.randint(len(far))]
    return np.exp2(a.ravel()).repeat(32)


def f64(x):
    return np.asarray(x).astype(np.float64)


E2M1 = np.array([0.0, 0.5, 1.0, 1.5, 2.0, 3.0, 4.0, 6.0, -0.0, -0.5, -1.0, -1.5, -2.0, -3.0, -4.0, -6.0])


def pack_weight(w, fmt):
    k, n = w.shape
    w = f64(np.asarray(w, np.float32).astype(ml_dtypes.bfloat16)).reshape(k // 32, 32, n)
    amax = np.abs(w).max(1)
    if fmt == "e4m3":
        byte = np.frexp(amax)[1] - 1 + 127 - 7
    else:
        mant, ex = np.frexp(amax / 6.0)
        byte = np.where(mant > 0.5, ex, ex - 1) + 127
    byte = np.clip(np.where(amax > 0, byte, 1), 1, 254)
    scaled = (w * np.exp2(127.0 - byte)[:, None, :]).reshape(k, n).astype(np.float32)
    by_word = np.ascontiguousarray(scaled.reshape(k // 512, 128, 4, n).transpose(0, 1, 3, 2))
    if fmt == "e4m3":
        words = by_word.astype(ml_dtypes.float8_e4m3fn).view(np.uint8)
    else:
        c = by_word.astype(ml_dtypes.float4_e2m1fn).view(np.uint8) & 0xF
        words = (c[..., 0::2] | (c[..., 1::2] << 4)).reshape(k // 512, 128, 2 * n)
    return np.ascontiguousarray(words), np.ascontiguousarray(byte.astype(np.uint8).reshape(k // 512, 16, n))


def unpack_weight(words, scales, fmt):
    g, _, n = scales.shape
    words = np.ascontiguousarray(words).reshape(g, 128, n, -1)
    if fmt == "e4m3":
        vals = words.view(ml_dtypes.float8_e4m3fn).astype(np.float64)
    else:
        nib = np.empty((g, 128, n, 4), np.uint8)
        nib[..., 0::2] = words & 0xF
        nib[..., 1::2] = words >> 4
        vals = E2M1[nib]
    vals = vals * np.repeat(np.exp2(scales.astype(np.float64) - 127.0), 8, axis=1)[..., None]
    return vals.transpose(0, 1, 3, 2).reshape(g * 512, n)


def planes(y):
    n, m = y.shape
    v = y.astype(np.float32).astype(ml_dtypes.bfloat16).astype(np.float64).reshape(n // 32, 32, m)
    top = np.abs(v).max(1)
    byte = np.clip(np.where(top > 0, np.frexp(top)[1] - 1 + 127 - 7, 1), 1, 254)
    codes = (v * np.exp2(127.0 - byte)[:, None, :]).reshape(n, m).astype(np.float32).astype(ml_dtypes.float8_e4m3fn).view(np.uint8)
    words = codes.reshape(n // 512, 128, 4, m).transpose(0, 1, 3, 2)
    return np.ascontiguousarray(words), np.ascontiguousarray(byte.astype(np.uint8).reshape(n // 512, 16, m))


def silu(v):
    return v / (1.0 + np.exp(-np.maximum(v, -700.0)))


K, R, M, T = 2048, 512, 1024, 512


def setup_inputs():
    n = np.random.standard_normal
    s = mx_kscale(K)[:, None]
    u = mx_kscale(R)[:, None]
    p_w4 = pack_weight(n((K, M)) / np.sqrt(K) / s, "e2m1")
    return {
        "x": (n((K, T)) * s).astype(np.float32),
        "w4_words": p_w4[0],
        "w4_scales": p_w4[1],
        "down": (n((K, R)) / np.sqrt(K) / s * u.T).astype(np.float32),
        "up": (0.5 * n((R, M)) / np.sqrt(R) / u).astype(np.float32),
        "b": (0.3 * n(1024)).astype(np.float32),
    }


def reference(x, w4_words, w4_scales, down, up, b):
    x_ = mxq(f64(x), 0, "e4m3")
    w4_ = unpack_weight(w4_words, w4_scales, "e2m1")
    down_ = mxq(f64(down), 0, "e4m3")
    up_ = mxq(f64(up), 0, "e4m3")
    h_ = mxq(down_.T @ x_, 0, "e4m3")
    y = w4_.T @ x_ + up_.T @ h_
    out_0 = silu(y + f64(b)[:, None])
    return (out_0,) + planes(out_0)

@@ -1,0 +1,274 @@
+from contextlib import ExitStack
+
+import concourse.mybir as mybir
+
+K, R, M, T = 2048, 512, 1024, 512
+FLOPS = 2 * K * R * T + 2 * K * M * T + 2 * R * M * T
+
+F32 = mybir.dt.float32
+BF16 = mybir.dt.bfloat16
+I32 = mybir.dt.int32
+U32 = mybir.dt.uint32
+U8 = mybir.dt.uint8
+E4M3 = mybir.dt.float8_e4m3fn_x4
+E2M1 = mybir.dt.float4_e2m1fn_x4
+SILU = mybir.ActivationFunctionType.Silu
+
+P = 128
+PACK = 4
+KP = P * PACK
+PASSES = K // KP
+HALVES = M // KP
+
+
+def tile_mix_lowrank_fm_pl_silu_kernel(tc, x, w4_words, w4_scales, down, up, b, out_0, out_1, out_2):
+    nc = tc.nc
+    with ExitStack() as ctx:
+        sb = ctx.enter_context(tc.tile_pool(name="sb", bufs=1))
+        ps = ctx.enter_context(tc.psum_pool(name="ps", bufs=1))
+        ctx.enter_context(tc.manual_schedule())
+
+        def tiles(name, count, shape, dtype):
+            return [sb.tile(shape, dtype, name=name + str(n), align_bytes=64) for n in range(count)]
+
+        x_raw = tiles("x_raw", PASSES, [P, PACK, T], F32)
+        x_grp = tiles("x_grp", PASSES, [P, T, PACK], BF16)
+        x_code = tiles("x_code", PASSES, [P, T], U32)
+        x_scale = tiles("x_scale", PASSES, [P, T], U8)
+        d_raw = tiles("d_raw", PASSES - 1, [P, PACK, R], F32)
+        d_last = tiles("d_last", 2, [P, PACK, R // 2], F32)
+        d_grp = tiles("d_grp", PASSES, [P, PACK, P, PACK], BF16)
+        d_code = tiles("d_code", PASSES, [P, R], U32)
+        d_scale = tiles("d_scale", PASSES, [P, R], U8)
+        u_raw = tiles("u_raw", 2 * HALVES, [P, PACK, KP // 2], F32)
+        u_grp = tiles("u_grp", HALVES, [P, PACK, P, PACK], BF16)
+        u_code = tiles("u_code", HALVES, [P, KP], U32)
+        u_scale = tiles("u_scale", HALVES, [P, KP], U8)
+        w_raw = tiles("w_raw", HALVES, [P, PASSES, 2 * KP], U8)
+        w_code = tiles("w_code", HALVES, [P, PASSES, PACK, 2 * P], U8)
+        ws_raw = tiles("ws_raw", 1, [P, PASSES, M], U8)[0]
+        w_scale = tiles("w_scale", HALVES, [P, PASSES, PACK, P], U8)
+        bias = tiles("bias", 1, [P, HALVES, PACK], F32)[0]
+        warm = tiles("warm", 1, [P, 1], F32)[0]
+        h_rows = tiles("h_rows", 1, [P, PACK, T], BF16)[0]
+        h_grp = tiles("h_grp", 1, [P, T, PACK], BF16)[0]
+        h_code = tiles("h_code", 1, [P, T], U32)[0]
+        h_scale = tiles("h_scale", 1, [P, T], U8)[0]
+        o_rows = tiles("o_rows", 2 * HALVES, [P, PACK, T // 2], F32)
+        o_grp = tiles("o_grp", 2 * HALVES, [P, T // 2, PACK], BF16)
+        o_code = tiles("o_code", HALVES, [P, T], U32)
+        o_scale = tiles("o_scale", HALVES, [P, T], U8)
+
+        def copy(on_vector, out, in_):
+            if on_vector:
+                nc.vector.tensor_copy(out=out, in_=in_)
+            else:
+                nc.scalar.copy(out=out, in_=in_)
+
+        def interleave(on_vector, grp, rows, c0, c1):
+            copy(
+                on_vector,
+                grp[:, c0:c1, :].rearrange("p (c i) j -> p c j i", i=4),
+                rows[:, :, c0:c1].rearrange("p j (c i) -> p c j i", i=4),
+            )
+
+        def deal(on_vector, grp, raw, m0, i0, i1):
+            count = raw.shape[2] // PACK
+            copy(
+                on_vector,
+                grp[:, i0:i1, m0 : m0 + count, :].rearrange("p i m j -> p m j i"),
+                raw[:].rearrange("p j (m i) -> p m j i", i=PACK)[:, :, :, i0:i1],
+            )
+
+        def quantize(code, scale, flat, c0, c1):
+            nc.vector.quantize_mx(out=code[:, c0:c1].bitcast(E4M3), scales=scale[:, c0:c1], in_=flat[:, PACK * c0 : PACK * c1])
+
+        def flat3(grp):
+            return grp[:].rearrange("p c j -> p (c j)")
+
+        def flat4(grp):
+            return grp[:].rearrange("p i m j -> p (i m j)")
+
+        def deal_words(a, g):
+            nc.vector.tensor_copy(
+                out=w_code[a][:, g, :, :].rearrange("p i (m e) -> p i m e", e=2),
+                in_=w_raw[a][:, g, :].rearrange("p (m i e) -> p i m e", i=PACK, e=2),
+            )
+
+        def deal_scales(a):
+            nc.vector.tensor_copy(
+                out=w_scale[a][:],
+                in_=ws_raw[:, :, a * KP : (a + 1) * KP].rearrange("p g (m i) -> p g i m", i=PACK),
+            )
+
+        def rows(src, g, c0, c1):
+            return src[g * KP : (g + 1) * KP, c0:c1].rearrange("(p j) c -> p j c", j=PACK)
+
+        def load_words(a):
+            nc.sync.dma_start(
+                out=w_raw[a][:].bitcast(I32),
+                in_=w4_words[:, :, a * 2 * KP : (a + 1) * 2 * KP].rearrange("g p n -> p g n").bitcast(I32),
+            )
+
+        def base_pass(acc, a, i, g):
+            nc.tensor.matmul_mx(
+                out=acc[:], lhsT=w_code[a][:, g, i, :].bitcast(E2M1), lhsT_scale=w_scale[a][:, g, i, :],
+                rhs=x_code[g][:].bitcast(E4M3), rhs_scale=x_scale[g][:], start=(g == 0), stop=False,
+            )
+
+        def down_pass(acc, i, g):
+            cols = slice(i * P, (i + 1) * P)
+            nc.tensor.matmul_mx(
+                out=acc[:], lhsT=d_code[g][:, cols].bitcast(E4M3), lhsT_scale=d_scale[g][:, cols],
+                rhs=x_code[g][:].bitcast(E4M3), rhs_scale=x_scale[g][:], start=(g == 0), stop=(g == PASSES - 1),
+            )
+
+        def up_pass(acc, a, i):
+            cols = slice(i * P, (i + 1) * P)
+            nc.tensor.matmul_mx(
+                out=acc[:], lhsT=u_code[a][:, cols].bitcast(E4M3), lhsT_scale=u_scale[a][:, cols],
+                rhs=h_code[:].bitcast(E4M3), rhs_scale=h_scale[:], start=False, stop=True,
+            )
+
+        def silu(acc, a, s):
+            for i in range(PACK):
+                nc.scalar.activation(
+                    out=o_rows[2 * a + s][:, i, :], in_=acc[i][:, s * 256 : (s + 1) * 256], func=SILU, bias=bias[:, a, i : i + 1]
+                )
+
+        def store_rows(a, s):
+            nc.sync.dma_start(out=rows(out_0, a, s * 256, (s + 1) * 256), in_=o_rows[2 * a + s][:])
+
+        def quantize_out(a, s):
+            cols = slice(s * 256, (s + 1) * 256)
+            nc.vector.quantize_mx(out=o_code[a][:, cols].bitcast(E4M3), scales=o_scale[a][:, cols], in_=flat3(o_grp[2 * a + s]))
+
+        def store_words(a, c0, c1):
+            nc.sync.dma_start(
+                out=out_1[a].rearrange("p t i -> p (t i)")[:, PACK * c0 : PACK * c1].bitcast(I32),
+                in_=o_code[a][:, c0:c1].bitcast(I32),
+            )
+
+        def store_scales(a):
+            for q in range(4):
+                queue = nc.sync if q % 2 == 0 else nc.scalar
+                queue.dma_start(
+                    out=out_2[a, 4 * q : 4 * q + 4, :].bitcast(I32),
+                    in_=o_scale[a][32 * q : 32 * q + 4, :].bitcast(I32),
+                )
+
+        nc.vector.memset(ws_raw[:].bitcast(I32), 0)
+        nc.scalar.dma_start(out=bias[:], in_=b.rearrange("(a p i) -> p a i", a=HALVES, i=PACK))
+        for r in range(4):
+            nc.scalar.dma_start(
+                out=ws_raw[r:P:32, :, :].bitcast(I32),
+                in_=w4_scales.rearrange("g (q r) n -> r q g n", r=4)[r].bitcast(I32),
+            )
+        for g in range(PASSES):
+            nc.sync.dma_start(out=x_raw[g][:], in_=rows(x, g, 0, T))
+            if g == 0:
+                load_words(0)
+            if g < PASSES - 1:
+                nc.sync.dma_start(out=d_raw[g][:], in_=rows(down, g, 0, R))
+            if g == 1:
+                load_words(1)
+        for s in range(2):
+            nc.sync.dma_start(out=d_last[s][:], in_=rows(down, PASSES - 1, s * 256, (s + 1) * 256))
+        for n in range(2 * HALVES):
+            nc.sync.dma_start(out=u_raw[n][:], in_=rows(up, 0, n * 256, (n + 1) * 256))
+
+        nc.scalar.activation(out=warm[:], in_=bias[:, 0, 0:1], func=SILU)
+
+        h_acc = [ps.tile([P, T], F32, name="h_acc" + str(i), tag="low" + str(i)) for i in range(PACK)]
+        y0 = [ps.tile([P, T], F32, name="y0_" + str(i), tag="high" + str(i)) for i in range(PACK)]
+
+        def passes(g):
+            for i in range(PACK):
+                base_pass(y0[i], 0, i, g)
+            for i in range(PACK):
+                down_pass(h_acc[i], i, g)
+
+        interleave(False, x_grp[0], x_raw[0], 0, 256)
+        interleave(True, x_grp[0], x_raw[0], 256, 512)
+        deal_scales(0)
+        quantize(x_code[0], x_scale[0], flat3(x_grp[0]), 0, T)
+        deal_words(0, 0)
+        deal_words(0, 1)
+        deal(False, d_grp[0], d_raw[0], 0, 2, 4)
+        deal(True, d_grp[0], d_raw[0], 0, 0, 2)
+        deal_words(0, 2)
+        quantize(d_code[0], d_scale[0], flat4(d_grp[0]), 0, R)
+        deal_words(0, 3)
+        deal_scales(1)
+        passes(0)
+        for g in (1, 2):
+            interleave(False, x_grp[g], x_raw[g], 0, T)
+            deal(False, d_grp[g], d_raw[g], 0, 2, 4)
+            deal(True, d_grp[g], d_raw[g], 0, 0, 2)
+            quantize(x_code[g], x_scale[g], flat3(x_grp[g]), 0, T)
+            quantize(d_code[g], d_scale[g], flat4(d_grp[g]), 0, R)
+            if g == 1:
+                for gw in range(PASSES):
+                    deal_words(1, gw)
+            passes(g)
+        g = PASSES - 1
+        interleave(False, x_grp[g], x_raw[g], 384, T)
+        interleave(True, x_grp[g], x_raw[g], 0, 384)
+        quantize(x_code[g], x_scale[g], flat3(x_grp[g]), 0, T)
+        for s in range(2):
+            deal(False, d_grp[g], d_last[s], 64 * s, 2, 4)
+            deal(True, d_grp[g], d_last[s], 64 * s, 0, 2)
+        for i in range(PACK):
+            quantize(d_code[g], d_scale[g], flat4(d_grp[g]), i * P, (i + 1) * P)
+        passes(g)
+
+        for i in range(PACK):
+            nc.scalar.copy(out=h_rows[:, i, :], in_=h_acc[i][:])
+        for s in range(2):
+            deal(True, u_grp[0], u_raw[s], 64 * s, 0, 4)
+        quantize(u_code[0], u_scale[0], flat4(u_grp[0]), 0, KP)
+        interleave(False, h_grp, h_rows, 320, T)
+        interleave(True, h_grp, h_rows, 0, 256)
+        interleave(True, h_grp, h_rows, 256, 320)
+        quantize(h_code, h_scale, flat3(h_grp), 0, 256)
+        quantize(h_code, h_scale, flat3(h_grp), 256, T)
+        deal(False, u_grp[1], u_raw[2], 0, 2, 4)
+        deal(True, u_grp[1], u_raw[2], 0, 0, 2)
+        deal(True, u_grp[1], u_raw[3], 64, 0, 4)
+        quantize(u_code[1], u_scale[1], flat4(u_grp[1]), 0, KP)
+
+        y1 = [ps.tile([P, T], F32, name="y1_" + str(i), tag="low" + str(i)) for i in range(PACK)]
+        late = [(i, g) for i in range(PACK) for g in range(PASSES)]
+        for i, g in late[:10]:
+            base_pass(y1[i], 1, i, g)
+        for i in range(PACK):
+            up_pass(y0[i], 0, i)
+        for i, g in late[10:14]:
+            base_pass(y1[i], 1, i, g)
+        for i in range(PACK - 1):
+            up_pass(y1[i], 1, i)
+        for i, g in late[14:]:
+            base_pass(y1[i], 1, i, g)
+        up_pass(y1[PACK - 1], 1, PACK - 1)
+
+        for s in range(2):
+            silu(y0, 0, s)
+            store_rows(0, s)
+        for s in range(2):
+            interleave(True, o_grp[s], o_rows[s], 0, 256)
+        for s in range(2):
+            quantize_out(0, s)
+        silu(y1, 1, 0)
+        store_rows(1, 0)
+        store_words(0, 0, T)
+        silu(y1, 1, 1)
+        interleave(True, o_grp[2], o_rows[2], 0, 256)
+        quantize_out(1, 0)
+        store_rows(1, 1)
+        store_words(1, 0, 256)
+        interleave(False, o_grp[3], o_rows[3], 160, 256)
+        store_scales(0)
+        interleave(True, o_grp[3], o_rows[3], 0, 160)
+        quantize_out(1, 1)
+        store_words(1, 256, T)
+        store_scales(1)

@@ -35,16 +35,15 @@ def tile_mix_lowrank_fm_pl_silu_kernel(tc, x, w4_words, w4_scales, down, up, b, 
         x_grp = tiles("x_grp", PASSES, [P, T, PACK], BF16)
         x_code = tiles("x_code", PASSES, [P, T], U32)
         x_scale = tiles("x_scale", PASSES, [P, T], U8)
-        d_raw = tiles("d_raw", PASSES - 1, [P, PACK, R], F32)
-        d_last = tiles("d_last", 2, [P, PACK, R // 2], F32)
+        d_raw = tiles("d_raw", PASSES, [P, PACK, R], F32)
         d_grp = tiles("d_grp", PASSES, [P, PACK, P, PACK], BF16)
         d_code = tiles("d_code", PASSES, [P, R], U32)
         d_scale = tiles("d_scale", PASSES, [P, R], U8)
-        u_raw = tiles("u_raw", 2 * HALVES, [P, PACK, KP // 2], F32)
+        u_raw = tiles("u_raw", HALVES, [P, PACK, KP], F32)
         u_grp = tiles("u_grp", HALVES, [P, PACK, P, PACK], BF16)
         u_code = tiles("u_code", HALVES, [P, KP], U32)
         u_scale = tiles("u_scale", HALVES, [P, KP], U8)
-        w_raw = tiles("w_raw", HALVES, [P, PASSES, 2 * KP], U8)
+        w_raw = tiles("w_raw", 2, [P, PASSES // 2, 2 * M], U8)
         w_code = tiles("w_code", HALVES, [P, PASSES, PACK, 2 * P], U8)
         ws_raw = tiles("ws_raw", 1, [P, PASSES, M], U8)[0]
         w_scale = tiles("w_scale", HALVES, [P, PASSES, PACK, P], U8)
@@ -54,10 +53,10 @@ def tile_mix_lowrank_fm_pl_silu_kernel(tc, x, w4_words, w4_scales, down, up, b, 
         h_grp = tiles("h_grp", 1, [P, T, PACK], BF16)[0]
         h_code = tiles("h_code", 1, [P, T], U32)[0]
         h_scale = tiles("h_scale", 1, [P, T], U8)[0]
-        o_rows = tiles("o_rows", 2 * HALVES, [P, PACK, T // 2], F32)
-        o_grp = tiles("o_grp", 2 * HALVES, [P, T // 2, PACK], BF16)
+        o_rows = tiles("o_rows", HALVES, [P, PACK, T], F32)
+        o_grp = tiles("o_grp", HALVES, [P, T, PACK], BF16)
         o_code = tiles("o_code", HALVES, [P, T], U32)
-        o_scale = tiles("o_scale", HALVES, [P, T], U8)
+        o_scale = tiles("o_scale", 1, [P, T], U8)[0]
 
         def copy(on_vector, out, in_):
             if on_vector:
@@ -72,12 +71,11 @@ def tile_mix_lowrank_fm_pl_silu_kernel(tc, x, w4_words, w4_scales, down, up, b, 
                 rows[:, :, c0:c1].rearrange("p j (c i) -> p c j i", i=4),
             )
 
-        def deal(on_vector, grp, raw, m0, i0, i1):
-            count = raw.shape[2] // PACK
+        def deal(on_vector, grp, raw, i0, i1, m0=0, m1=P):
             copy(
                 on_vector,
-                grp[:, i0:i1, m0 : m0 + count, :].rearrange("p i m j -> p m j i"),
-                raw[:].rearrange("p j (m i) -> p m j i", i=PACK)[:, :, :, i0:i1],
+                grp[:, i0:i1, m0:m1, :].rearrange("p i m j -> p m j i"),
+                raw[:].rearrange("p j (m i) -> p m j i", i=PACK)[:, m0:m1, :, i0:i1],
             )
 
         def quantize(code, scale, flat, c0, c1):
@@ -92,7 +90,7 @@ def tile_mix_lowrank_fm_pl_silu_kernel(tc, x, w4_words, w4_scales, down, up, b, 
         def deal_words(a, g):
             nc.vector.tensor_copy(
                 out=w_code[a][:, g, :, :].rearrange("p i (m e) -> p i m e", e=2),
-                in_=w_raw[a][:, g, :].rearrange("p (m i e) -> p i m e", i=PACK, e=2),
+                in_=w_raw[g // 2][:, g % 2, a * 2 * KP : (a + 1) * 2 * KP].rearrange("p (m i e) -> p i m e", i=PACK, e=2),
             )
 
         def deal_scales(a):
@@ -104,10 +102,10 @@ def tile_mix_lowrank_fm_pl_silu_kernel(tc, x, w4_words, w4_scales, down, up, b, 
         def rows(src, g, c0, c1):
             return src[g * KP : (g + 1) * KP, c0:c1].rearrange("(p j) c -> p j c", j=PACK)
 
-        def load_words(a):
+        def load_words(n):
             nc.sync.dma_start(
-                out=w_raw[a][:].bitcast(I32),
-                in_=w4_words[:, :, a * 2 * KP : (a + 1) * 2 * KP].rearrange("g p n -> p g n").bitcast(I32),
+                out=w_raw[n][:].bitcast(I32),
+                in_=w4_words[2 * n : 2 * n + 2].rearrange("g p n -> p g n").bitcast(I32),
             )
 
         def base_pass(acc, a, i, g):
@@ -130,52 +128,45 @@ def tile_mix_lowrank_fm_pl_silu_kernel(tc, x, w4_words, w4_scales, down, up, b, 
                 rhs=h_code[:].bitcast(E4M3), rhs_scale=h_scale[:], start=False, stop=True,
             )
 
-        def silu(acc, a, s):
-            for i in range(PACK):
-                nc.scalar.activation(
-                    out=o_rows[2 * a + s][:, i, :], in_=acc[i][:, s * 256 : (s + 1) * 256], func=SILU, bias=bias[:, a, i : i + 1]
-                )
+        def silu(acc, a, i, c0, c1):
+            nc.scalar.activation(out=o_rows[a][:, i, c0:c1], in_=acc[i][:, c0:c1], func=SILU, bias=bias[:, a, i : i + 1])
 
-        def store_rows(a, s):
-            nc.sync.dma_start(out=rows(out_0, a, s * 256, (s + 1) * 256), in_=o_rows[2 * a + s][:])
+        def store_rows(a, i0, i1):
+            nc.sync.dma_start(out=rows(out_0, a, 0, T)[:, i0:i1, :], in_=o_rows[a][:, i0:i1, :])
 
-        def quantize_out(a, s):
-            cols = slice(s * 256, (s + 1) * 256)
-            nc.vector.quantize_mx(out=o_code[a][:, cols].bitcast(E4M3), scales=o_scale[a][:, cols], in_=flat3(o_grp[2 * a + s]))
+        def quantize_out(a, c0, c1):
+            nc.vector.quantize_mx(
+                out=o_code[a][:, c0:c1].bitcast(E4M3), scales=o_scale[4 * a : P, c0:c1], in_=flat3(o_grp[a])[:, PACK * c0 : PACK * c1]
+            )
 
-        def store_words(a, c0, c1):
-            nc.sync.dma_start(
+        def store_words(queue, a, c0, c1):
+            queue.dma_start(
                 out=out_1[a].rearrange("p t i -> p (t i)")[:, PACK * c0 : PACK * c1].bitcast(I32),
                 in_=o_code[a][:, c0:c1].bitcast(I32),
             )
 
-        def store_scales(a):
+        def store_scales():
             for q in range(4):
-                queue = nc.sync if q % 2 == 0 else nc.scalar
+                queue = nc.sync if q % 2 else nc.scalar
                 queue.dma_start(
-                    out=out_2[a, 4 * q : 4 * q + 4, :].bitcast(I32),
-                    in_=o_scale[a][32 * q : 32 * q + 4, :].bitcast(I32),
+                    out=out_2[:, 4 * q : 4 * q + 4, :].bitcast(I32),
+                    in_=o_scale[32 * q : 32 * q + 8, :].bitcast(I32),
                 )
 
         nc.vector.memset(ws_raw[:].bitcast(I32), 0)
         nc.scalar.dma_start(out=bias[:], in_=b.rearrange("(a p i) -> p a i", a=HALVES, i=PACK))
+        load_words(0)
+        load_words(1)
         for r in range(4):
-            nc.scalar.dma_start(
+            nc.sync.dma_start(
                 out=ws_raw[r:P:32, :, :].bitcast(I32),
                 in_=w4_scales.rearrange("g (q r) n -> r q g n", r=4)[r].bitcast(I32),
             )
         for g in range(PASSES):
             nc.sync.dma_start(out=x_raw[g][:], in_=rows(x, g, 0, T))
-            if g == 0:
-                load_words(0)
-            if g < PASSES - 1:
-                nc.sync.dma_start(out=d_raw[g][:], in_=rows(down, g, 0, R))
-            if g == 1:
-                load_words(1)
-        for s in range(2):
-            nc.sync.dma_start(out=d_last[s][:], in_=rows(down, PASSES - 1, s * 256, (s + 1) * 256))
-        for n in range(2 * HALVES):
-            nc.sync.dma_start(out=u_raw[n][:], in_=rows(up, 0, n * 256, (n + 1) * 256))
+            nc.sync.dma_start(out=d_raw[g][:], in_=rows(down, g, 0, R))
+        for a in range(HALVES):
+            nc.sync.dma_start(out=u_raw[a][:], in_=rows(up, 0, a * KP, (a + 1) * KP))
 
         nc.scalar.activation(out=warm[:], in_=bias[:, 0, 0:1], func=SILU)
 
@@ -188,87 +179,81 @@ def tile_mix_lowrank_fm_pl_silu_kernel(tc, x, w4_words, w4_scales, down, up, b, 
             for i in range(PACK):
                 down_pass(h_acc[i], i, g)
 
-        interleave(False, x_grp[0], x_raw[0], 0, 256)
-        interleave(True, x_grp[0], x_raw[0], 256, 512)
+        for g in range(PASSES):
+            deal_words(0, g)
         deal_scales(0)
-        quantize(x_code[0], x_scale[0], flat3(x_grp[0]), 0, T)
-        deal_words(0, 0)
-        deal_words(0, 1)
-        deal(False, d_grp[0], d_raw[0], 0, 2, 4)
-        deal(True, d_grp[0], d_raw[0], 0, 0, 2)
-        deal_words(0, 2)
-        quantize(d_code[0], d_scale[0], flat4(d_grp[0]), 0, R)
-        deal_words(0, 3)
-        deal_scales(1)
-        passes(0)
-        for g in (1, 2):
+        later = {0: [lambda: deal_scales(1), lambda: deal_words(1, 0)], 1: [lambda: deal_words(1, 1), lambda: deal_words(1, 2)], 2: [lambda: deal_words(1, 3)]}
+        for g in range(PASSES - 1):
             interleave(False, x_grp[g], x_raw[g], 0, T)
-            deal(False, d_grp[g], d_raw[g], 0, 2, 4)
-            deal(True, d_grp[g], d_raw[g], 0, 0, 2)
+            for job in later[g]:
+                job()
             quantize(x_code[g], x_scale[g], flat3(x_grp[g]), 0, T)
+            deal(False, d_grp[g], d_raw[g], 2, 4)
+            deal(True, d_grp[g], d_raw[g], 0, 2)
             quantize(d_code[g], d_scale[g], flat4(d_grp[g]), 0, R)
-            if g == 1:
-                for gw in range(PASSES):
-                    deal_words(1, gw)
             passes(g)
         g = PASSES - 1
-        interleave(False, x_grp[g], x_raw[g], 384, T)
-        interleave(True, x_grp[g], x_raw[g], 0, 384)
+        interleave(False, x_grp[g], x_raw[g], 320, T)
+        interleave(True, x_grp[g], x_raw[g], 0, 320)
         quantize(x_code[g], x_scale[g], flat3(x_grp[g]), 0, T)
-        for s in range(2):
-            deal(False, d_grp[g], d_last[s], 64 * s, 2, 4)
-            deal(True, d_grp[g], d_last[s], 64 * s, 0, 2)
+        deal(False, d_grp[g], d_raw[g], 2, 4)
+        deal(True, d_grp[g], d_raw[g], 0, 2)
         for i in range(PACK):
             quantize(d_code[g], d_scale[g], flat4(d_grp[g]), i * P, (i + 1) * P)
         passes(g)
 
         for i in range(PACK):
-            nc.scalar.copy(out=h_rows[:, i, :], in_=h_acc[i][:])
-        for s in range(2):
-            deal(True, u_grp[0], u_raw[s], 64 * s, 0, 4)
-        quantize(u_code[0], u_scale[0], flat4(u_grp[0]), 0, KP)
-        interleave(False, h_grp, h_rows, 320, T)
+            copy(i % 2 == 1, h_rows[:, i, :], h_acc[i][:])
+        deal(False, u_grp[0], u_raw[0], 0, 2)
+        interleave(False, h_grp, h_rows, 384, T)
         interleave(True, h_grp, h_rows, 0, 256)
-        interleave(True, h_grp, h_rows, 256, 320)
+        interleave(True, h_grp, h_rows, 256, 384)
         quantize(h_code, h_scale, flat3(h_grp), 0, 256)
+        quantize(u_code[0], u_scale[0], flat4(u_grp[0]), 0, P)
         quantize(h_code, h_scale, flat3(h_grp), 256, T)
-        deal(False, u_grp[1], u_raw[2], 0, 2, 4)
-        deal(True, u_grp[1], u_raw[2], 0, 0, 2)
-        deal(True, u_grp[1], u_raw[3], 64, 0, 4)
-        quantize(u_code[1], u_scale[1], flat4(u_grp[1]), 0, KP)
+        quantize(u_code[0], u_scale[0], flat4(u_grp[0]), P, 2 * P)
+        deal(False, u_grp[0], u_raw[0], 2, 4)
+        deal(True, u_grp[1], u_raw[1], 0, 2)
+        quantize(u_code[0], u_scale[0], flat4(u_grp[0]), 2 * P, KP)
+        deal(True, u_grp[1], u_raw[1], 2, 4)
+        quantize(u_code[1], u_scale[1], flat4(u_grp[1]), 0, 256)
+        quantize(u_code[1], u_scale[1], flat4(u_grp[1]), 256, KP)
 
         y1 = [ps.tile([P, T], F32, name="y1_" + str(i), tag="low" + str(i)) for i in range(PACK)]
         late = [(i, g) for i in range(PACK) for g in range(PASSES)]
         for i, g in late[:10]:
             base_pass(y1[i], 1, i, g)
+        up_pass(y0[0], 0, 0)
+        up_pass(y0[1], 0, 1)
+        for i, g in late[10:12]:
+            base_pass(y1[i], 1, i, g)
+        up_pass(y0[2], 0, 2)
+        up_pass(y0[3], 0, 3)
+        base_pass(y1[3], 1, 3, 0)
         for i in range(PACK):
-            up_pass(y0[i], 0, i)
-        for i, g in late[10:14]:
-            base_pass(y1[i], 1, i, g)
-        for i in range(PACK - 1):
             up_pass(y1[i], 1, i)
-        for i, g in late[14:]:
-            base_pass(y1[i], 1, i, g)
-        up_pass(y1[PACK - 1], 1, PACK - 1)
+            if i < PACK - 1:
+                base_pass(y1[3], 1, 3, i + 1)
 
-        for s in range(2):
-            silu(y0, 0, s)
-            store_rows(0, s)
-        for s in range(2):
-            interleave(True, o_grp[s], o_rows[s], 0, 256)
-        for s in range(2):
-            quantize_out(0, s)
-        silu(y1, 1, 0)
-        store_rows(1, 0)
-        store_words(0, 0, T)
-        silu(y1, 1, 1)
-        interleave(True, o_grp[2], o_rows[2], 0, 256)
-        quantize_out(1, 0)
-        store_rows(1, 1)
-        store_words(1, 0, 256)
-        interleave(False, o_grp[3], o_rows[3], 160, 256)
-        store_scales(0)
-        interleave(True, o_grp[3], o_rows[3], 0, 160)
-        quantize_out(1, 1)
-        store_words(1, 256, T)
-        store_scales(1)
+        for i in range(PACK):
+            silu(y0, 0, i, 0, T)
+            store_rows(0, i, i + 1)
+        interleave(True, o_grp[0], o_rows[0], 0, 256)
+        interleave(True, o_grp[0], o_rows[0], 256, T)
+        quantize_out(0, 0, 256)
+        quantize_out(0, 256, T)
+        for i in range(PACK - 1):
+            silu(y1, 1, i, 0, T)
+            store_rows(1, i, i + 1)
+        store_words(nc.sync, 0, 0, T)
+        silu(y1, 1, PACK - 1, 0, 256)
+        silu(y1, 1, PACK - 1, 256, T)
+        store_rows(1, PACK - 1, PACK)
+        interleave(True, o_grp[1], o_rows[1], 0, 256)
+        interleave(False, o_grp[1], o_rows[1], 384, T)
+        interleave(True, o_grp[1], o_rows[1], 256, 384)
+        quantize_out(1, 0, 256)
+        store_words(nc.sync, 1, 0, 256)
+        quantize_out(1, 256, T)
+        store_words(nc.sync, 1, 256, T)
+        store_scales()

@@ -19,6 +19,7 @@ PACK = 4
 KP = P * PACK
 PASSES = K // KP
 HALVES = M // KP
+LAST_CUT = 384
 
 
 def tile_mix_lowrank_fm_pl_silu_kernel(tc, x, w4_words, w4_scales, down, up, b, out_0, out_1, out_2):
@@ -31,11 +32,14 @@ def tile_mix_lowrank_fm_pl_silu_kernel(tc, x, w4_words, w4_scales, down, up, b, 
         def tiles(name, count, shape, dtype):
             return [sb.tile(shape, dtype, name=name + str(n), align_bytes=64) for n in range(count)]
 
-        x_raw = tiles("x_raw", PASSES, [P, PACK, T], F32)
+        x_head = tiles("x_head", 1, [P, 2, PACK, T], F32)[0]
+        x_raw = [x_head[:, 0], x_head[:, 1]] + tiles("x_raw", 2, [P, PACK, T], F32)
         x_grp = tiles("x_grp", PASSES, [P, T, PACK], BF16)
         x_code = tiles("x_code", PASSES, [P, T], U32)
         x_scale = tiles("x_scale", PASSES, [P, T], U8)
-        d_raw = tiles("d_raw", PASSES, [P, PACK, R], F32)
+        d_head = tiles("d_head", 1, [P, 2, PACK, R], F32)[0]
+        d_raw = [d_head[:, 0], d_head[:, 1]] + tiles("d_raw", 1, [P, PACK, R], F32)
+        d_last = [sb.tile([P, PACK, width], F32, name="d_last" + str(width), align_bytes=64) for width in (LAST_CUT, R - LAST_CUT)]
         d_grp = tiles("d_grp", PASSES, [P, PACK, P, PACK], BF16)
         d_code = tiles("d_code", PASSES, [P, R], U32)
         d_scale = tiles("d_scale", PASSES, [P, R], U8)
@@ -43,7 +47,7 @@ def tile_mix_lowrank_fm_pl_silu_kernel(tc, x, w4_words, w4_scales, down, up, b, 
         u_grp = tiles("u_grp", HALVES, [P, PACK, P, PACK], BF16)
         u_code = tiles("u_code", HALVES, [P, KP], U32)
         u_scale = tiles("u_scale", HALVES, [P, KP], U8)
-        w_raw = tiles("w_raw", 2, [P, PASSES // 2, 2 * M], U8)
+        w_raw = tiles("w_raw", 1, [P, PASSES, 2 * M], U8)[0]
         w_code = tiles("w_code", HALVES, [P, PASSES, PACK, 2 * P], U8)
         ws_raw = tiles("ws_raw", 1, [P, PASSES, M], U8)[0]
         w_scale = tiles("w_scale", HALVES, [P, PASSES, PACK, P], U8)
@@ -71,11 +75,12 @@ def tile_mix_lowrank_fm_pl_silu_kernel(tc, x, w4_words, w4_scales, down, up, b, 
                 rows[:, :, c0:c1].rearrange("p j (c i) -> p c j i", i=4),
             )
 
-        def deal(on_vector, grp, raw, i0, i1, m0=0, m1=P):
+        def deal(on_vector, grp, raw, i0, i1, m0=0):
+            count = raw.shape[2] // PACK
             copy(
                 on_vector,
-                grp[:, i0:i1, m0:m1, :].rearrange("p i m j -> p m j i"),
-                raw[:].rearrange("p j (m i) -> p m j i", i=PACK)[:, m0:m1, :, i0:i1],
+                grp[:, i0:i1, m0 : m0 + count, :].rearrange("p i m j -> p m j i"),
+                raw[:].rearrange("p j (m i) -> p m j i", i=PACK)[:, :, :, i0:i1],
             )
 
         def quantize(code, scale, flat, c0, c1):
@@ -90,7 +95,7 @@ def tile_mix_lowrank_fm_pl_silu_kernel(tc, x, w4_words, w4_scales, down, up, b, 
         def deal_words(a, g):
             nc.vector.tensor_copy(
                 out=w_code[a][:, g, :, :].rearrange("p i (m e) -> p i m e", e=2),
-                in_=w_raw[g // 2][:, g % 2, a * 2 * KP : (a + 1) * 2 * KP].rearrange("p (m i e) -> p i m e", i=PACK, e=2),
+                in_=w_raw[:, g, a * 2 * KP : (a + 1) * 2 * KP].rearrange("p (m i e) -> p i m e", i=PACK, e=2),
             )
 
         def deal_scales(a):
@@ -101,12 +106,6 @@ def tile_mix_lowrank_fm_pl_silu_kernel(tc, x, w4_words, w4_scales, down, up, b, 
 
         def rows(src, g, c0, c1):
             return src[g * KP : (g + 1) * KP, c0:c1].rearrange("(p j) c -> p j c", j=PACK)
-
-        def load_words(n):
-            nc.sync.dma_start(
-                out=w_raw[n][:].bitcast(I32),
-                in_=w4_words[2 * n : 2 * n + 2].rearrange("g p n -> p g n").bitcast(I32),
-            )
 
         def base_pass(acc, a, i, g):
             nc.tensor.matmul_mx(
@@ -154,21 +153,27 @@ def tile_mix_lowrank_fm_pl_silu_kernel(tc, x, w4_words, w4_scales, down, up, b, 
                 )
 
         nc.vector.memset(ws_raw[:].bitcast(I32), 0)
-        nc.scalar.dma_start(out=bias[:], in_=b.rearrange("(a p i) -> p a i", a=HALVES, i=PACK))
-        load_words(0)
-        load_words(1)
+        nc.gpsimd.memset(warm[:], 0.0)
+        nc.sync.dma_start(out=w_raw[:].bitcast(I32), in_=w4_words.rearrange("g p n -> p g n").bitcast(I32))
         for r in range(4):
-            nc.sync.dma_start(
+            nc.scalar.dma_start(
                 out=ws_raw[r:P:32, :, :].bitcast(I32),
                 in_=w4_scales.rearrange("g (q r) n -> r q g n", r=4)[r].bitcast(I32),
             )
-        for g in range(PASSES):
+        nc.sync.dma_start(out=x_head[:], in_=x[0 : 2 * KP, :].rearrange("(g p j) c -> p g j c", g=2, j=PACK))
+        nc.sync.dma_start(out=d_head[:], in_=down[0 : 2 * KP, :].rearrange("(g p j) c -> p g j c", g=2, j=PACK))
+        for g in range(2, PASSES):
             nc.sync.dma_start(out=x_raw[g][:], in_=rows(x, g, 0, T))
-            nc.sync.dma_start(out=d_raw[g][:], in_=rows(down, g, 0, R))
+            if g < PASSES - 1:
+                nc.sync.dma_start(out=d_raw[g][:], in_=rows(down, g, 0, R))
+        nc.sync.dma_start(out=d_last[0][:], in_=rows(down, PASSES - 1, 0, LAST_CUT))
+        nc.sync.dma_start(out=d_last[1][:], in_=rows(down, PASSES - 1, LAST_CUT, R))
         for a in range(HALVES):
             nc.sync.dma_start(out=u_raw[a][:], in_=rows(up, 0, a * KP, (a + 1) * KP))
+            if a == 0:
+                nc.sync.dma_start(out=bias[:], in_=b.rearrange("(a p i) -> p a i", a=HALVES, i=PACK))
 
-        nc.scalar.activation(out=warm[:], in_=bias[:, 0, 0:1], func=SILU)
+        nc.scalar.activation(out=warm[:], in_=warm[:], func=SILU)
 
         h_acc = [ps.tile([P, T], F32, name="h_acc" + str(i), tag="low" + str(i)) for i in range(PACK)]
         y0 = [ps.tile([P, T], F32, name="y0_" + str(i), tag="high" + str(i)) for i in range(PACK)]
@@ -179,25 +184,40 @@ def tile_mix_lowrank_fm_pl_silu_kernel(tc, x, w4_words, w4_scales, down, up, b, 
             for i in range(PACK):
                 down_pass(h_acc[i], i, g)
 
-        for g in range(PASSES):
-            deal_words(0, g)
-        deal_scales(0)
-        later = {0: [lambda: deal_scales(1), lambda: deal_words(1, 0)], 1: [lambda: deal_words(1, 1), lambda: deal_words(1, 2)], 2: [lambda: deal_words(1, 3)]}
-        for g in range(PASSES - 1):
+        for a in range(HALVES):
+            for g in range(PASSES):
+                deal_words(a, g)
+        for a in range(HALVES):
+            deal_scales(a)
+        for g in range(2):
             interleave(False, x_grp[g], x_raw[g], 0, T)
-            for job in later[g]:
-                job()
             quantize(x_code[g], x_scale[g], flat3(x_grp[g]), 0, T)
+        for g in range(2):
             deal(False, d_grp[g], d_raw[g], 2, 4)
             deal(True, d_grp[g], d_raw[g], 0, 2)
+        for g in range(2):
             quantize(d_code[g], d_scale[g], flat4(d_grp[g]), 0, R)
-            passes(g)
+        for g in range(2):
+            for i in range(PACK):
+                base_pass(y0[i], 0, i, g)
+        for g in range(2):
+            for i in range(PACK):
+                down_pass(h_acc[i], i, g)
+        g = 2
+        interleave(False, x_grp[g], x_raw[g], 256, T)
+        interleave(True, x_grp[g], x_raw[g], 0, 256)
+        quantize(x_code[g], x_scale[g], flat3(x_grp[g]), 0, T)
+        deal(False, d_grp[g], d_raw[g], 2, 4)
+        deal(True, d_grp[g], d_raw[g], 0, 2)
+        quantize(d_code[g], d_scale[g], flat4(d_grp[g]), 0, R)
+        passes(g)
         g = PASSES - 1
         interleave(False, x_grp[g], x_raw[g], 320, T)
         interleave(True, x_grp[g], x_raw[g], 0, 320)
         quantize(x_code[g], x_scale[g], flat3(x_grp[g]), 0, T)
-        deal(False, d_grp[g], d_raw[g], 2, 4)
-        deal(True, d_grp[g], d_raw[g], 0, 2)
+        for part, m0 in ((0, 0), (1, LAST_CUT // PACK)):
+            deal(False, d_grp[g], d_last[part], 2, 4, m0)
+            deal(True, d_grp[g], d_last[part], 0, 2, m0)
         for i in range(PACK):
             quantize(d_code[g], d_scale[g], flat4(d_grp[g]), i * P, (i + 1) * P)
         passes(g)

from contextlib import ExitStack

import concourse.mybir as mybir

K, R, M, T = 2048, 512, 1024, 512
FLOPS = 2 * K * R * T + 2 * K * M * T + 2 * R * M * T

F32 = mybir.dt.float32
BF16 = mybir.dt.bfloat16
I32 = mybir.dt.int32
U32 = mybir.dt.uint32
U8 = mybir.dt.uint8
E4M3 = mybir.dt.float8_e4m3fn_x4
E2M1 = mybir.dt.float4_e2m1fn_x4
SILU = mybir.ActivationFunctionType.Silu

P = 128
PACK = 4
KP = P * PACK
PASSES = K // KP
HALVES = M // KP
LAST_CUT = 384


def tile_mix_lowrank_fm_pl_silu_kernel(tc, x, w4_words, w4_scales, down, up, b, out_0, out_1, out_2):
    nc = tc.nc
    with ExitStack() as ctx:
        sb = ctx.enter_context(tc.tile_pool(name="sb", bufs=1))
        ps = ctx.enter_context(tc.psum_pool(name="ps", bufs=1))
        ctx.enter_context(tc.manual_schedule())

        def tiles(name, count, shape, dtype):
            return [sb.tile(shape, dtype, name=name + str(n), align_bytes=64) for n in range(count)]

        x_head = tiles("x_head", 1, [P, 2, PACK, T], F32)[0]
        x_raw = [x_head[:, 0], x_head[:, 1]] + tiles("x_raw", 2, [P, PACK, T], F32)
        x_grp = tiles("x_grp", PASSES, [P, T, PACK], BF16)
        x_code = tiles("x_code", PASSES, [P, T], U32)
        x_scale = tiles("x_scale", PASSES, [P, T], U8)
        d_head = tiles("d_head", 1, [P, 2, PACK, R], F32)[0]
        d_raw = [d_head[:, 0], d_head[:, 1]] + tiles("d_raw", 1, [P, PACK, R], F32)
        d_last = [sb.tile([P, PACK, width], F32, name="d_last" + str(width), align_bytes=64) for width in (LAST_CUT, R - LAST_CUT)]
        d_grp = tiles("d_grp", PASSES, [P, PACK, P, PACK], BF16)
        d_code = tiles("d_code", PASSES, [P, R], U32)
        d_scale = tiles("d_scale", PASSES, [P, R], U8)
        u_raw = tiles("u_raw", HALVES, [P, PACK, KP], F32)
        u_grp = tiles("u_grp", HALVES, [P, PACK, P, PACK], BF16)
        u_code = tiles("u_code", HALVES, [P, KP], U32)
        u_scale = tiles("u_scale", HALVES, [P, KP], U8)
        w_raw = tiles("w_raw", 1, [P, PASSES, 2 * M], U8)[0]
        w_code = tiles("w_code", HALVES, [P, PASSES, PACK, 2 * P], U8)
        ws_raw = tiles("ws_raw", 1, [P, PASSES, M], U8)[0]
        w_scale = tiles("w_scale", HALVES, [P, PASSES, PACK, P], U8)
        bias = tiles("bias", 1, [P, HALVES, PACK], F32)[0]
        warm = tiles("warm", 1, [P, 1], F32)[0]
        h_rows = tiles("h_rows", 1, [P, PACK, T], BF16)[0]
        h_grp = tiles("h_grp", 1, [P, T, PACK], BF16)[0]
        h_code = tiles("h_code", 1, [P, T], U32)[0]
        h_scale = tiles("h_scale", 1, [P, T], U8)[0]
        o_rows = tiles("o_rows", HALVES, [P, PACK, T], F32)
        o_grp = tiles("o_grp", HALVES, [P, T, PACK], BF16)
        o_code = tiles("o_code", HALVES, [P, T], U32)
        o_scale = tiles("o_scale", 1, [P, T], U8)[0]

        def copy(on_vector, out, in_):
            if on_vector:
                nc.vector.tensor_copy(out=out, in_=in_)
            else:
                nc.scalar.copy(out=out, in_=in_)

        def interleave(on_vector, grp, rows, c0, c1):
            copy(
                on_vector,
                grp[:, c0:c1, :].rearrange("p (c i) j -> p c j i", i=4),
                rows[:, :, c0:c1].rearrange("p j (c i) -> p c j i", i=4),
            )

        def deal(on_vector, grp, raw, i0, i1, m0=0):
            count = raw.shape[2] // PACK
            copy(
                on_vector,
                grp[:, i0:i1, m0 : m0 + count, :].rearrange("p i m j -> p m j i"),
                raw[:].rearrange("p j (m i) -> p m j i", i=PACK)[:, :, :, i0:i1],
            )

        def quantize(code, scale, flat, c0, c1):
            nc.vector.quantize_mx(out=code[:, c0:c1].bitcast(E4M3), scales=scale[:, c0:c1], in_=flat[:, PACK * c0 : PACK * c1])

        def flat3(grp):
            return grp[:].rearrange("p c j -> p (c j)")

        def flat4(grp):
            return grp[:].rearrange("p i m j -> p (i m j)")

        def deal_words(a, g):
            nc.vector.tensor_copy(
                out=w_code[a][:, g, :, :].rearrange("p i (m e) -> p i m e", e=2),
                in_=w_raw[:, g, a * 2 * KP : (a + 1) * 2 * KP].rearrange("p (m i e) -> p i m e", i=PACK, e=2),
            )

        def deal_scales(a):
            nc.vector.tensor_copy(
                out=w_scale[a][:],
                in_=ws_raw[:, :, a * KP : (a + 1) * KP].rearrange("p g (m i) -> p g i m", i=PACK),
            )

        def rows(src, g, c0, c1):
            return src[g * KP : (g + 1) * KP, c0:c1].rearrange("(p j) c -> p j c", j=PACK)

        def base_pass(acc, a, i, g):
            nc.tensor.matmul_mx(
                out=acc[:], lhsT=w_code[a][:, g, i, :].bitcast(E2M1), lhsT_scale=w_scale[a][:, g, i, :],
                rhs=x_code[g][:].bitcast(E4M3), rhs_scale=x_scale[g][:], start=(g == 0), stop=False,
            )

        def down_pass(acc, i, g):
            cols = slice(i * P, (i + 1) * P)
            nc.tensor.matmul_mx(
                out=acc[:], lhsT=d_code[g][:, cols].bitcast(E4M3), lhsT_scale=d_scale[g][:, cols],
                rhs=x_code[g][:].bitcast(E4M3), rhs_scale=x_scale[g][:], start=(g == 0), stop=(g == PASSES - 1),
            )

        def up_pass(acc, a, i):
            cols = slice(i * P, (i + 1) * P)
            nc.tensor.matmul_mx(
                out=acc[:], lhsT=u_code[a][:, cols].bitcast(E4M3), lhsT_scale=u_scale[a][:, cols],
                rhs=h_code[:].bitcast(E4M3), rhs_scale=h_scale[:], start=False, stop=True,
            )

        def silu(acc, a, i, c0, c1):
            nc.scalar.activation(out=o_rows[a][:, i, c0:c1], in_=acc[i][:, c0:c1], func=SILU, bias=bias[:, a, i : i + 1])

        def store_rows(a, i0, i1):
            nc.sync.dma_start(out=rows(out_0, a, 0, T)[:, i0:i1, :], in_=o_rows[a][:, i0:i1, :])

        def quantize_out(a, c0, c1):
            nc.vector.quantize_mx(
                out=o_code[a][:, c0:c1].bitcast(E4M3), scales=o_scale[4 * a : P, c0:c1], in_=flat3(o_grp[a])[:, PACK * c0 : PACK * c1]
            )

        def store_words(queue, a, c0, c1):
            queue.dma_start(
                out=out_1[a].rearrange("p t i -> p (t i)")[:, PACK * c0 : PACK * c1].bitcast(I32),
                in_=o_code[a][:, c0:c1].bitcast(I32),
            )

        def store_scales():
            for q in range(4):
                queue = nc.sync if q % 2 else nc.scalar
                queue.dma_start(
                    out=out_2[:, 4 * q : 4 * q + 4, :].bitcast(I32),
                    in_=o_scale[32 * q : 32 * q + 8, :].bitcast(I32),
                )

        nc.vector.memset(ws_raw[:].bitcast(I32), 0)
        nc.gpsimd.memset(warm[:], 0.0)
        nc.sync.dma_start(out=w_raw[:].bitcast(I32), in_=w4_words.rearrange("g p n -> p g n").bitcast(I32))
        for r in range(4):
            nc.scalar.dma_start(
                out=ws_raw[r:P:32, :, :].bitcast(I32),
                in_=w4_scales.rearrange("g (q r) n -> r q g n", r=4)[r].bitcast(I32),
            )
        nc.sync.dma_start(out=x_head[:], in_=x[0 : 2 * KP, :].rearrange("(g p j) c -> p g j c", g=2, j=PACK))
        nc.sync.dma_start(out=d_head[:], in_=down[0 : 2 * KP, :].rearrange("(g p j) c -> p g j c", g=2, j=PACK))
        for g in range(2, PASSES):
            nc.sync.dma_start(out=x_raw[g][:], in_=rows(x, g, 0, T))
            if g < PASSES - 1:
                nc.sync.dma_start(out=d_raw[g][:], in_=rows(down, g, 0, R))
        nc.sync.dma_start(out=d_last[0][:], in_=rows(down, PASSES - 1, 0, LAST_CUT))
        nc.sync.dma_start(out=d_last[1][:], in_=rows(down, PASSES - 1, LAST_CUT, R))
        for a in range(HALVES):
            nc.sync.dma_start(out=u_raw[a][:], in_=rows(up, 0, a * KP, (a + 1) * KP))
            if a == 0:
                nc.sync.dma_start(out=bias[:], in_=b.rearrange("(a p i) -> p a i", a=HALVES, i=PACK))

        nc.scalar.activation(out=warm[:], in_=warm[:], func=SILU)

        h_acc = [ps.tile([P, T], F32, name="h_acc" + str(i), tag="low" + str(i)) for i in range(PACK)]
        y0 = [ps.tile([P, T], F32, name="y0_" + str(i), tag="high" + str(i)) for i in range(PACK)]

        def passes(g):
            for i in range(PACK):
                base_pass(y0[i], 0, i, g)
            for i in range(PACK):
                down_pass(h_acc[i], i, g)

        for a in range(HALVES):
            for g in range(PASSES):
                deal_words(a, g)
        for a in range(HALVES):
            deal_scales(a)
        for g in range(2):
            interleave(False, x_grp[g], x_raw[g], 0, T)
            quantize(x_code[g], x_scale[g], flat3(x_grp[g]), 0, T)
        for g in range(2):
            deal(False, d_grp[g], d_raw[g], 2, 4)
            deal(True, d_grp[g], d_raw[g], 0, 2)
        for g in range(2):
            quantize(d_code[g], d_scale[g], flat4(d_grp[g]), 0, R)
        for g in range(2):
            for i in range(PACK):
                base_pass(y0[i], 0, i, g)
        for g in range(2):
            for i in range(PACK):
                down_pass(h_acc[i], i, g)
        g = 2
        interleave(False, x_grp[g], x_raw[g], 256, T)
        interleave(True, x_grp[g], x_raw[g], 0, 256)
        quantize(x_code[g], x_scale[g], flat3(x_grp[g]), 0, T)
        deal(False, d_grp[g], d_raw[g], 2, 4)
        deal(True, d_grp[g], d_raw[g], 0, 2)
        quantize(d_code[g], d_scale[g], flat4(d_grp[g]), 0, R)
        passes(g)
        g = PASSES - 1
        interleave(False, x_grp[g], x_raw[g], 320, T)
        interleave(True, x_grp[g], x_raw[g], 0, 320)
        quantize(x_code[g], x_scale[g], flat3(x_grp[g]), 0, T)
        for part, m0 in ((0, 0), (1, LAST_CUT // PACK)):
            deal(False, d_grp[g], d_last[part], 2, 4, m0)
            deal(True, d_grp[g], d_last[part], 0, 2, m0)
        for i in range(PACK):
            quantize(d_code[g], d_scale[g], flat4(d_grp[g]), i * P, (i + 1) * P)
        passes(g)

        for i in range(PACK):
            copy(i % 2 == 1, h_rows[:, i, :], h_acc[i][:])
        deal(False, u_grp[0], u_raw[0], 0, 2)
        interleave(False, h_grp, h_rows, 384, T)
        interleave(True, h_grp, h_rows, 0, 256)
        interleave(True, h_grp, h_rows, 256, 384)
        quantize(h_code, h_scale, flat3(h_grp), 0, 256)
        quantize(u_code[0], u_scale[0], flat4(u_grp[0]), 0, P)
        quantize(h_code, h_scale, flat3(h_grp), 256, T)
        quantize(u_code[0], u_scale[0], flat4(u_grp[0]), P, 2 * P)
        deal(False, u_grp[0], u_raw[0], 2, 4)
        deal(True, u_grp[1], u_raw[1], 0, 2)
        quantize(u_code[0], u_scale[0], flat4(u_grp[0]), 2 * P, KP)
        deal(True, u_grp[1], u_raw[1], 2, 4)
        quantize(u_code[1], u_scale[1], flat4(u_grp[1]), 0, 256)
        quantize(u_code[1], u_scale[1], flat4(u_grp[1]), 256, KP)

        y1 = [ps.tile([P, T], F32, name="y1_" + str(i), tag="low" + str(i)) for i in range(PACK)]
        late = [(i, g) for i in range(PACK) for g in range(PASSES)]
        for i, g in late[:10]:
            base_pass(y1[i], 1, i, g)
        up_pass(y0[0], 0, 0)
        up_pass(y0[1], 0, 1)
        for i, g in late[10:12]:
            base_pass(y1[i], 1, i, g)
        up_pass(y0[2], 0, 2)
        up_pass(y0[3], 0, 3)
        base_pass(y1[3], 1, 3, 0)
        for i in range(PACK):
            up_pass(y1[i], 1, i)
            if i < PACK - 1:
                base_pass(y1[3], 1, 3, i + 1)

        for i in range(PACK):
            silu(y0, 0, i, 0, T)
            store_rows(0, i, i + 1)
        interleave(True, o_grp[0], o_rows[0], 0, 256)
        interleave(True, o_grp[0], o_rows[0], 256, T)
        quantize_out(0, 0, 256)
        quantize_out(0, 256, T)
        for i in range(PACK - 1):
            silu(y1, 1, i, 0, T)
            store_rows(1, i, i + 1)
        store_words(nc.sync, 0, 0, T)
        silu(y1, 1, PACK - 1, 0, 256)
        silu(y1, 1, PACK - 1, 256, T)
        store_rows(1, PACK - 1, PACK)
        interleave(True, o_grp[1], o_rows[1], 0, 256)
        interleave(False, o_grp[1], o_rows[1], 384, T)
        interleave(True, o_grp[1], o_rows[1], 256, 384)
        quantize_out(1, 0, 256)
        store_words(nc.sync, 1, 0, 256)
        quantize_out(1, 256, T)
        store_words(nc.sync, 1, 256, T)
        store_scales()
